import numpy as np, ml_dtypes
CORES = [5,29,101,125,133,157,229,253]
N = 8
TK, LAY = 512, 3
def setup_inputs(rng):
    return {"x": rng.standard_normal((N, 128, TK), dtype=np.float32).astype(ml_dtypes.bfloat16), "wu": (rng.standard_normal((N, 128, LAY * 256), dtype=np.float32) / 16).astype(ml_dtypes.bfloat16), "wd": (rng.standard_normal((N, 128, 256), dtype=np.float32) / 16).astype(ml_dtypes.bfloat16)}
def setup_inputs_big(rng):
    d = setup_inputs(rng)
    for k in ("x",): d[k] = (d[k].astype(np.float32) * 1048576.0).astype(d[k].dtype)
    return d
def setup_inputs_small(rng):
    d = setup_inputs(rng)
    for k in ("x",): d[k] = (d[k].astype(np.float32) * (1 / 1048576.0)).astype(d[k].dtype)
    return d
def setup_inputs_apart(rng):
    d = setup_inputs(rng)
    f = (10.0 ** rng.permutation(np.linspace(-1.5, 1.5, N))).astype(np.float32).reshape(N, 1, 1)
    for k in ("x",): d[k] = (d[k].astype(np.float32) * f).astype(d[k].dtype)
    return d
def reference(x, wu, wd):
    X, WU, WD = x.astype(np.float64), wu.astype(np.float64), wd.astype(np.float64)
    s = list(X)
    for l in range(LAY):
        for q in range(0, N, 2 << l):
            p = q + (1 << l)
            s[q] = np.maximum(WU[q][:, 256 * l:256 * l + 128].T @ s[q] + WU[q][:, 256 * l + 128:256 * l + 256].T @ s[p], 0.0)
    for l in range(LAY - 1, -1, -1):
        for q in range(0, N, 2 << l):
            p = q + (1 << l)
            s[p] = np.maximum(WD[p][:, 0:128].T @ s[p] + WD[p][:, 128:256].T @ s[q], 0.0)
    return {"y": np.stack(s).astype(ml_dtypes.bfloat16)}

from concourse.bass import DstId, RemoteDMATransfer
from concourse.mybir import AluOpType

TK, HF = 512, 256
NODES = ["a0", "a1", "b", "c", "y4", "ye", "yo"]
SCRATCH = {
    "X": ("sbuf", [128, 4 * TK], "bfloat16"),
    "WA": ("sbuf", [128, 512], "bfloat16"),
    "WB": ("sbuf", [128, 256], "bfloat16"),
    "WC": ("sbuf", [128, 256], "bfloat16"),
    "WD": ("sbuf", [128, 256], "bfloat16"),
    "WE": ("sbuf", [128, 256], "bfloat16"),
    "WO": ("sbuf", [128, 256], "bfloat16"),
    "A0": ("sbuf", [128, TK], "bfloat16"),
    "A1": ("sbuf", [128, TK], "bfloat16"),
    "BO": ("sbuf", [128, TK], "bfloat16"),
    "BP": ("sbuf", [128, TK], "bfloat16"),
    "C0": ("sbuf", [128, TK], "bfloat16"),
    "Y4": ("sbuf", [128, TK], "bfloat16"),
    "YE": ("sbuf", [128, TK], "bfloat16"),
    "YO": ("sbuf", [128, TK], "bfloat16"),
    "ZERO": ("sbuf", [128, HF], "float32"),
}
for _i in range(8):
    SCRATCH["P%d" % _i] = ("psum", [128, 512], "float32")
SEMAPHORES = (["sX0", "sX1", "sX2", "sX3", "sWA", "sWB", "sWC", "sWD", "sWE", "sWO", "sBP", "snd", "st0", "st1", "vz"]
              + ["m_%s%d" % (n, h) for n in NODES for h in (0, 1)] + ["v_%s%d" % (n, h) for n in NODES for h in (0, 1)])


def _pop(mask):
    return bin(mask).count("1")


def _outgoing(r):
    q1, j = r - r % 4, r % 4
    out = [("X%d" % j, "hx", [r ^ 1, r ^ 3, r ^ 2], True)]
    if j == 0:
        out.append(("WA", "hw", [q1 + 3, q1 + 1, q1 + 2], True))
        if r == 0:
            out.append(("WC", "hw", [3, 7, 2, 6, 1, 5, 4], False))
        else:
            out.append(("WD", "hw", [q1 + 3, q1 + 2, q1 + 1], False))
    if j == 2:
        out.append(("WB", "hw", [q1 + 1, q1 + 3, q1], True))
        out.append(("WE", "hw", [q1 + 3], False))
    return out


def _relays(T, topo, r):
    cores = list(T.cores)
    c = cores[r]
    total = topo.CORES_PER_HOST * (max(topo.host(k) for k in cores) + 1)
    far = [d for d in cores if d != c and not topo.may_write(c, d)]
    own = [h for h in range(total) if topo.host(h) == topo.host(c) and topo.chip(h) == topo.chip(c) and h not in cores
           and all(topo.may_write(h, d) for d in far)]
    same = [h for h in own if topo.die(h) == topo.die(c)]
    other = [h for h in own if topo.die(h) != topo.die(c)]
    return {"hx": same[0], "hw": (other + same[1:])[0]}


def rank_program(g, core, T, topo):
    cores = list(T.cores)
    sent = [0]

    def ap(buf):
        if buf[0] == "X":
            i = int(buf[1])
            return T.X[:, TK * i:TK * (i + 1)]
        return T[buf][:]

    def send(src, dst, sem, dests, mask):
        if len(dests) == 1:
            rid, pid = topo.addr(dests[0], core)
            g.remote_dma(out_ap=dst, in_ap=src, remote_sem=sem, local_sem=T.sem.snd, pid=pid, routing_id=rid,
                         dma_engine_mask=mask)
        else:
            ids = []
            for d in dests:
                rid, pid = topo.addr(d, core)
                ids.append(DstId(rid=rid, pnc=pid))
            g.remote_dma_fused([RemoteDMATransfer(dst_ids=ids, dma_engine_mask=mask, remote_sem=sem, srcs=[src],
                                                  dsts=[dst for _ in dests], alu_op=0)], local_sem=T.sem.snd)
        sent[0] += _pop(mask)

    rank = T.rank_of(core)

    if rank is None:
        for r in range(len(cores)):
            rel = _relays(T, topo, r)
            for role in ("hx", "hw"):
                if rel[role] != core:
                    continue
                src = cores[r]
                lo = topo.mask(src, cores[r ^ 2])
                hi = topo.mask(src, core) & ~lo
                k = 0
                for buf, ro, dests, urgent in _outgoing(r):
                    if ro != role:
                        continue
                    far = [cores[d] for d in dests if not topo.may_write(src, cores[d])]
                    if not far:
                        continue
                    lane = lo if (role == "hw" and urgent) else hi
                    g.wait_ge(T.sem["s" + buf], _pop(lane))
                    if urgent:
                        for d in far:
                            send(ap(buf), ap(buf), T.sem["s" + buf], [d], topo.mask(core, d))
                    else:
                        send(ap(buf), ap(buf), T.sem["s" + buf], far, topo.mask(core, far[0]))
                    k += 1
        if sent[0]:
            g.wait_ge(T.sem.snd, sent[0])
        return

    r = rank
    G, q1, j = r // 4, r - r % 4, r % 4
    rel = _relays(T, topo, r)
    lo = topo.mask(core, cores[r ^ 2])
    hi = topo.mask(core, rel["hx"]) & ~lo

    g.vector.memset(T.ZERO[:], 0.0).then_inc(T.sem.vz, 1)
    g.sync.dma_start(ap("X%d" % j), T.x[:, :]).then_inc(T.sem["sX%d" % j], 16)
    if j == 0:
        g.scalar.dma_start(T.WA[:], T.wu[:, 0:512]).then_inc(T.sem.sWA, 16)
        if r == 0:
            g.sync.dma_start(T.WC[:], T.wu[:, 512:768]).then_inc(T.sem.sWC, 16)
        else:
            g.sync.dma_start(T.WD[:], T.wd[:, :]).then_inc(T.sem.sWD, 16)
    elif j == 2:
        g.scalar.dma_start(T.WB[:], T.wu[:, 0:256]).then_inc(T.sem.sWB, 16)
        g.sync.dma_start(T.WE[:], T.wd[:, :]).then_inc(T.sem.sWE, 16)
    else:
        g.scalar.dma_start(T.WO[:], T.wd[:, :]).then_inc(T.sem.sWO, 16)

    owner = {"WA": q1, "WB": q1 + 2, "WC": 0, "WD": 4, "WE": q1 + 2, "WO": r}
    for i in range(4):
        owner["X%d" % i] = q1 + i

    def full(buf):
        s = owner[buf]
        if s == r:
            return 16
        sender = cores[s] if topo.may_write(cores[s], core) else _relays(T, topo, s)["hx" if buf[0] == "X" else "hw"]
        return _pop(topo.mask(sender, core))

    out = _outgoing(r)
    split = []
    for buf, role, dests, urgent in out:
        near = [cores[d] for d in dests if topo.may_write(core, cores[d])]
        far = [cores[d] for d in dests if not topo.may_write(core, cores[d])]
        split.append((buf, role, near, far, urgent))
    for urgent_now in (True, False):
        for buf, role, near, far, urgent in split:
            if urgent == urgent_now and far:
                g.wait_ge(T.sem["s" + buf], 16)
                send(ap(buf), ap(buf), T.sem["s" + buf], [rel[role]], lo if (role == "hw" and urgent) else hi)
        for buf, role, near, far, urgent in split:
            if urgent == urgent_now and near:
                g.wait_ge(T.sem["s" + buf], 16)
                send(ap(buf), ap(buf), T.sem["s" + buf], near, lo)

    nodes = {
        "a0": ("A0", [("WA", 0, "X0"), ("WA", 128, "X1")]),
        "a1": ("A1", [("WB", 0, "X2"), ("WB", 128, "X3")]),
        "b": ("BO", [("WA", 256, "A0"), ("WA", 384, "A1")]),
        "c": ("C0", [("WC", 0, "BP" if G else "BO"), ("WC", 128, "BO" if G else "BP")]),
    }
    top = "C0"
    chain = ["c"]
    if G:
        nodes["y4"] = ("Y4", [("WD", 0, "BO"), ("WD", 128, top)])
        top = "Y4"
        chain.append("y4")
    if j >= 2:
        nodes["ye"] = ("YE", [("WE", 0, "A1"), ("WE", 128, top)])
        top = "YE"
        chain.append("ye")
    if j % 2:
        nodes["yo"] = ("YO", [("WO", 0, "X%d" % j), ("WO", 128, top)])
        top = "YO"
        chain.append("yo")
    maker = {}
    for n in nodes:
        maker[nodes[n][0]] = n

    waited = {}

    def need(q, qn, sem, val):
        if waited.get((qn, sem), 0) < val:
            q.wait_ge(T.sem[sem], val)
            waited[(qn, sem)] = val

    free = list(range(8))
    retired = []
    banks = {}
    opened = {}

    def mm(n, t):
        W, off, src = nodes[n][1][t]
        first = n not in opened
        for h in (0, 1):
            dep = None
            if first:
                if free:
                    banks[(n, h)] = free.pop(0)
                else:
                    banks[(n, h)], dep = retired.pop(0)
            need(g.tensor, "t", "s" + W, full(W))
            if src[0] == "X":
                need(g.tensor, "t", "s" + src, full(src))
                rhs = T.X[:, TK * int(src[1]) + HF * h:TK * int(src[1]) + HF * (h + 1)]
            else:
                if src == "BP":
                    need(g.tensor, "t", "sBP", _pop(topo.mask(cores[r ^ 4], core)))
                else:
                    need(g.tensor, "t", "v_%s%d" % (maker[src], h), 1)
                rhs = T[src][:, HF * h:HF * (h + 1)]
            if dep:
                need(g.tensor, "t", dep, 1)
            g.tensor.matmul(T["P%d" % banks[(n, h)]][:, 0:HF], T[W][:, off:off + 128], rhs, first,
                            not first).then_inc(T.sem["m_%s%d" % (n, h)], 1)
        if not first and n in ("a0", "a1", "b"):
            for h in (0, 1):
                retired.append((banks[(n, h)], "v_%s%d" % (n, h)))
        opened[n] = True

    ex = {j: 0.0, j ^ 2: 4.0, j ^ 1: 6.0, j ^ 3: 7.0}
    ew = {"WA": {0: 0.0, 2: 5.0, 3: 6.1, 1: 7.1}[j], "WB": {2: 0.0, 0: 5.0, 1: 5.5, 3: 5.9}[j]}
    if j % 2:
        mm("yo", 0)
    terms = sorted((max(ew["WA" if k == 0 else "WB"], ex[2 * k + t]), k, t) for k in (0, 1) for t in (0, 1))
    k_last = terms[3][1]
    k_first = 1 - k_last
    done_first = max(e for e, k, t in terms if k == k_first)
    ahead = max(done_first + 0.3, ew["WA"]) < terms[3][0]
    for e, k, t in terms[:3]:
        mm("a%d" % k, t)
    if ahead:
        mm("b", k_first)
    mm("a%d" % k_last, terms[3][2])
    if not ahead:
        mm("b", k_first)
    mm("b", k_last)
    mm("c", 1 if G else 0)
    if "ye" in nodes:
        mm("ye", 0)
    if "y4" in nodes:
        mm("y4", 0)
    mm("c", 0 if G else 1)
    for n in chain[1:]:
        mm(n, 1)

    g.vector.wait_ge(T.sem.vz, 1)
    for n in ["a%d" % k_first, "a%d" % k_last, "b"] + chain:
        for h in (0, 1):
            g.vector.wait_ge(T.sem["m_%s%d" % (n, h)], 2)
            g.vector.tensor_tensor(T[nodes[n][0]][:, HF * h:HF * (h + 1)], T["P%d" % banks[(n, h)]][:, 0:HF], T.ZERO[:],
                                   AluOpType.max).then_inc(T.sem["v_%s%d" % (n, h)], 1)

    g.wait_ge(T.sem.v_b0, 1)
    g.wait_ge(T.sem.v_b1, 1)
    send(T.BO[:], T.BP[:], T.sem.sBP, [cores[r ^ 4]], lo)

    last = chain[-1]
    g.sync.wait_ge(T.sem["v_%s0" % last], 1)
    g.sync.dma_start(T.y[:, 0:HF], T[top][:, 0:HF]).then_inc(T.sem.st0, 16)
    g.scalar.wait_ge(T.sem["v_%s1" % last], 1)
    g.scalar.dma_start(T.y[:, HF:TK], T[top][:, HF:TK]).then_inc(T.sem.st1, 16)
    g.wait_ge(T.sem.snd, sent[0])
    g.wait_ge(T.sem.st0, 16)
    g.wait_ge(T.sem.st1, 16)
